import numpy as np, ml_dtypes
CORES = [120,124,248,252,376,380,504,508]
N = 8
NH, QP = 8, 32
def setup_inputs(rng):
    return {"q": rng.standard_normal((N, 128, NH * QP), dtype=np.float32).astype(ml_dtypes.bfloat16), "k": rng.standard_normal((N, 128, NH * 128), dtype=np.float32).astype(ml_dtypes.bfloat16), "v": rng.standard_normal((N, 128, NH * 128), dtype=np.float32).astype(ml_dtypes.bfloat16)}
def setup_inputs_big(rng):
    d = setup_inputs(rng)
    for k in ("q", "k", "v"): d[k] = (d[k].astype(np.float32) * 1024.0).astype(d[k].dtype)
    return d
def setup_inputs_small(rng):
    d = setup_inputs(rng)
    for k in ("q", "k", "v"): d[k] = (d[k].astype(np.float32) * (1 / 1024.0)).astype(d[k].dtype)
    return d
def setup_inputs_apart(rng):
    d = setup_inputs(rng)
    f = (10.0 ** rng.permutation(np.linspace(-1.5, 1.5, N))).astype(np.float32).reshape(N, 1, 1)
    for k in ("q", "k", "v"): d[k] = (d[k].astype(np.float32) * f).astype(d[k].dtype)
    return d
def reference(q, k, v):
    Q, K, V = q.astype(np.float64), k.astype(np.float64), v.astype(np.float64)
    y = np.zeros((N, 128, NH * QP))
    for r in range(N):
        for h in range(NH):
            for j in range(N):
                S = np.maximum(K[j][:, 128 * h:128 * h + 128].T @ Q[r][:, QP * h:QP * h + QP], 0.0)
                y[r][:, QP * h:QP * h + QP] += V[j][:, 128 * h:128 * h + 128].T @ S
    return {"y": y.astype(ml_dtypes.bfloat16 if q.dtype != np.float64 else np.float64)}

@@ -1,0 +1,152 @@
+from concourse.bass import DstId, RemoteDMATransfer
+from concourse.mybir import AluOpType
+
+NH, QP, KP = 8, 32, 128
+W = NH * QP
+BF, F32 = "bfloat16", "float32"
+
+SCRATCH = {
+    "qall": ("sbuf", [128, 4, W], BF),
+    "k0": ("sbuf", [128, NH * KP], BF), "v0": ("sbuf", [128, NH * KP], BF),
+    "k1": ("sbuf", [128, NH * KP], BF), "v1": ("sbuf", [128, NH * KP], BF),
+    "zeros": ("sbuf", [128, NH, 2, QP], F32),
+    "sE0": ("sbuf", [128, NH, 2, QP], BF), "sE1": ("sbuf", [128, NH, 2, QP], BF),
+    "sL0": ("sbuf", [128, 4, 2, QP], BF), "sL1": ("sbuf", [128, 4, 2, QP], BF),
+    "sL2": ("sbuf", [128, 4, 2, QP], BF), "sL3": ("sbuf", [128, 4, 2, QP], BF),
+    "ob_s": ("sbuf", [128, W], BF), "ob_x": ("sbuf", [128, W], BF), "ob_d": ("sbuf", [128, W], BF),
+    "rawland": ("sbuf", [128, W], BF), "dland": ("sbuf", [128, W], BF), "fland": ("sbuf", [128, W], BF),
+    "ybuf": ("sbuf", [128, W], BF),
+    "qd": ("dram", [128, W], BF),
+    "qxd": ("dram", [128, W], BF),
+    "psE0": ("psum", [128, NH, 2, QP], F32), "psE1": ("psum", [128, NH, 2, QP], F32),
+    "psL0": ("psum", [128, NH, 2, QP], F32), "psL1": ("psum", [128, NH, 2, QP], F32),
+    "psL2": ("psum", [128, NH, 2, QP], F32), "psL3": ("psum", [128, NH, 2, QP], F32),
+    "psOL": ("psum", [128, 2, W], F32), "psOE": ("psum", [128, 2, W], F32),
+}
+SEMAPHORES = [
+    "ld_qd", "ld_q", "ld_k", "ld_v", "ld_qx", "st_y",
+    "a_qx", "a_qs", "a_qd", "a_k", "a_v", "a_raw", "a_d", "a_f", "lsem", "z",
+    "pE0", "pE1", "rE0", "rE1", "pL0", "pL1", "pL2", "pL3", "rL0", "rL1", "rL2", "rL3",
+    "pOL", "pOE", "c_d", "c_x", "c_s", "t1", "fin",
+]
+
+
+def _bits(mask):
+    return bin(mask).count("1")
+
+
+def rank_program(g, core, T, topo):
+    if T.rank_of(core) is None:
+        return
+    sem = T.sem
+    sib = [c for c in T.cores if c != core and topo.host(c) == topo.host(core) and topo.chip(c) == topo.chip(core)][0]
+    far = [c for c in T.cores if topo.host(c) != topo.host(core) and topo.die(c) == topo.die(core)]
+    S = [c for c in far if topo.same_plane(core, c)][0]
+    X = [c for c in far if topo.may_write(core, c) and not topo.same_plane(core, c)][0]
+    sent = [0]
+
+    def send(dst, out_ap, in_ap, rsem):
+        rid, pid = topo.addr(dst, core)
+        m = topo.mask(core, dst)
+        g.remote_dma(out_ap, in_ap, rsem, sem.lsem, pid, rid, m)
+        sent[0] += _bits(m)
+        return _bits(m)
+
+    n_off = _bits(topo.mask(core, X))
+    n_on = _bits(topo.mask(core, sib))
+
+    g.sync.dma_start(T.qd[:], T.q[:]).then_inc(sem.ld_qd, 16)
+    g.scalar.dma_start(T.k0[:], T.k[:]).then_inc(sem.ld_k, 16)
+    g.sync.dma_start(T.qall[:, 0], T.q[:]).then_inc(sem.ld_q, 16)
+    g.sync.dma_start(T.v0[:], T.v[:]).then_inc(sem.ld_v, 16)
+    g.vector.memset(T.zeros[:], 0.0).then_inc(sem.z, 1)
+
+    g.wait_ge(sem.ld_qd, 16)
+    send(X, T.qxd[:], T.qd[:], sem.a_qx)
+    send(S, T.qall[:, 1], T.qd[:], sem.a_qs)
+    g.wait_ge(sem.ld_k, 16)
+    send(sib, T.k1[:], T.k0[:], sem.a_k)
+    g.wait_ge(sem.ld_v, 16)
+    send(sib, T.v1[:], T.v0[:], sem.a_v)
+    g.wait_ge(sem.a_qx, n_off)
+    send(S, T.qall[:, 3], T.qxd[:], sem.a_qd)
+    g.sync.wait_ge(sem.a_qx, n_off)
+    g.sync.dma_start(T.qall[:, 2], T.qxd[:]).then_inc(sem.ld_qx, 16)
+
+    te, ve = g.tensor, g.vector
+    ks, vs = (T.k0, T.k1), (T.v0, T.v1)
+    psE, sE, pE, rE = (T.psE0, T.psE1), (T.sE0, T.sE1), (sem.pE0, sem.pE1), (sem.rE0, sem.rE1)
+    psL = (T.psL0, T.psL1, T.psL2, T.psL3)
+    sL = (T.sL0, T.sL1, T.sL2, T.sL3)
+    pL = (sem.pL0, sem.pL1, sem.pL2, sem.pL3)
+    rL = (sem.rL0, sem.rL1, sem.rL2, sem.rL3)
+
+    def hk(h):
+        return slice(KP * h, KP * h + KP)
+
+    def hq(h):
+        return slice(QP * h, QP * h + QP)
+
+    te.wait_ge(sem.ld_q, 16)
+    te.wait_ge(sem.a_qs, n_off)
+    te.wait_ge(sem.ld_k, 16)
+    for j in range(2):
+        if j == 1:
+            te.wait_ge(sem.a_k, n_on)
+        for h in range(NH):
+            te.matmul(psE[j][:, h], ks[j][:, hk(h)], T.qall[:, 0:2, hq(h)], True, True).then_inc(pE[j], 1)
+    te.wait_ge(sem.ld_qx, 16)
+    te.wait_ge(sem.a_qd, n_off)
+    for p in range(4):
+        for hh in range(2):
+            h = 2 * p + hh
+            for j in range(2):
+                te.matmul(psL[p][:, 2 * hh + j], ks[j][:, hk(h)], T.qall[:, 2:4, hq(h)], True, True).then_inc(pL[p], 1)
+    te.wait_ge(sem.ld_v, 16)
+    te.wait_ge(sem.a_v, n_on)
+    for p in range(4):
+        te.wait_ge(rL[p], 1)
+        for hh in range(2):
+            h = 2 * p + hh
+            for j in range(2):
+                te.matmul(T.psOL[:, 0:2, hq(h)], vs[j][:, hk(h)], sL[p][:, 2 * hh + j], j == 0, j == 1).then_inc(sem.pOL, 1)
+    te.wait_ge(sem.rE0, 1)
+    te.wait_ge(sem.rE1, 1)
+    for h in range(NH):
+        for j in range(2):
+            te.matmul(T.psOE[:, 0:2, hq(h)], vs[j][:, hk(h)], sE[j][:, h], j == 0, j == 1).then_inc(sem.pOE, 1)
+
+    ve.wait_ge(sem.z, 1)
+    for j in range(2):
+        ve.wait_ge(pE[j], NH)
+        ve.tensor_tensor(sE[j][:], psE[j][:], T.zeros[:], AluOpType.max).then_inc(rE[j], 1)
+    for p in range(4):
+        ve.wait_ge(pL[p], 4)
+        ve.tensor_tensor(sL[p][:], psL[p][:, 0:4], T.zeros[:, 0:4], AluOpType.max).then_inc(rL[p], 1)
+    ve.wait_ge(sem.pOL, 2 * NH)
+    ve.tensor_copy(T.ob_d[:], T.psOL[:, 1]).then_inc(sem.c_d, 1)
+    ve.tensor_copy(T.ob_x[:], T.psOL[:, 0]).then_inc(sem.c_x, 1)
+    ve.wait_ge(sem.pOE, 2 * NH)
+    ve.tensor_copy(T.ob_s[:], T.psOE[:, 1]).then_inc(sem.c_s, 1)
+    ve.wait_ge(sem.a_d, n_off)
+    ve.tensor_tensor(T.psOE[:, 0], T.psOE[:, 0], T.dland[:], AluOpType.add).then_inc(sem.t1, 1)
+    ve.wait_ge(sem.t1, 1)
+    ve.wait_ge(sem.a_f, n_off)
+    ve.tensor_tensor(T.ybuf[:], T.psOE[:, 0], T.fland[:], AluOpType.add).then_inc(sem.fin, 1)
+
+    g.wait_ge(sem.c_d, 1)
+    send(S, T.rawland[:], T.ob_d[:], sem.a_raw)
+    g.wait_ge(sem.c_s, 1)
+    send(S, T.dland[:], T.ob_s[:], sem.a_d)
+    g.wait_ge(sem.c_x, 1)
+    g.wait_ge(sem.a_raw, n_off)
+    rid, pid = topo.addr(X, core)
+    g.remote_dma_fused([RemoteDMATransfer(dst_ids=[DstId(rid=rid, pnc=pid)], dma_engine_mask=topo.mask(core, X),
+                                          remote_sem=sem.a_f, srcs=[T.rawland[:], T.ob_x[:]], dsts=[T.fland[:]],
+                                          alu_op=1)], local_sem=sem.lsem)
+    sent[0] += n_off
+
+    g.sync.wait_ge(sem.fin, 1)
+    g.sync.dma_start(T.y[:], T.ybuf[:]).then_inc(sem.st_y, 16)
+    g.sync.wait_ge(sem.st_y, 16)
+    g.wait_ge(sem.lsem, sent[0])

@@ -3,6 +3,7 @@ from concourse.mybir import AluOpType
 
 NH, QP, KP = 8, 32, 128
 W = NH * QP
+HH = NH // 2
 BF, F32 = "bfloat16", "float32"
 
 SCRATCH = {
@@ -13,26 +14,32 @@ SCRATCH = {
     "sE0": ("sbuf", [128, NH, 2, QP], BF), "sE1": ("sbuf", [128, NH, 2, QP], BF),
     "sL0": ("sbuf", [128, 4, 2, QP], BF), "sL1": ("sbuf", [128, 4, 2, QP], BF),
     "sL2": ("sbuf", [128, 4, 2, QP], BF), "sL3": ("sbuf", [128, 4, 2, QP], BF),
-    "ob_s": ("sbuf", [128, W], BF), "ob_x": ("sbuf", [128, W], BF), "ob_d": ("sbuf", [128, W], BF),
-    "rawland": ("sbuf", [128, W], BF), "dland": ("sbuf", [128, W], BF), "fland": ("sbuf", [128, W], BF),
-    "ybuf": ("sbuf", [128, W], BF),
+    "ob_s": ("sbuf", [128, NH, QP], BF), "ob_x": ("sbuf", [128, NH, QP], BF), "ob_d": ("sbuf", [128, NH, QP], BF),
+    "rawland": ("sbuf", [128, NH, QP], BF), "dland": ("sbuf", [128, NH, QP], BF), "fland": ("sbuf", [128, NH, QP], BF),
+    "ybuf": ("sbuf", [128, NH, QP], BF),
     "qd": ("dram", [128, W], BF),
     "qxd": ("dram", [128, W], BF),
     "psE0": ("psum", [128, NH, 2, QP], F32), "psE1": ("psum", [128, NH, 2, QP], F32),
     "psL0": ("psum", [128, NH, 2, QP], F32), "psL1": ("psum", [128, NH, 2, QP], F32),
     "psL2": ("psum", [128, NH, 2, QP], F32), "psL3": ("psum", [128, NH, 2, QP], F32),
-    "psOL": ("psum", [128, 2, W], F32), "psOE": ("psum", [128, 2, W], F32),
+    "psOL": ("psum", [128, NH, 2, QP], F32), "psOE": ("psum", [128, NH, 2, QP], F32),
 }
 SEMAPHORES = [
     "ld_qd", "ld_q", "ld_k", "ld_v", "ld_qx", "st_y",
-    "a_qx", "a_qs", "a_qd", "a_k", "a_v", "a_raw", "a_d", "a_f", "lsem", "z",
+    "a_qx", "a_qs", "a_qd", "a_k", "a_v", "a_raw0", "a_raw1", "a_d", "a_f0", "a_f1", "lsem", "z",
     "pE0", "pE1", "rE0", "rE1", "pL0", "pL1", "pL2", "pL3", "rL0", "rL1", "rL2", "rL3",
-    "pOL", "pOE", "c_d", "c_x", "c_s", "t1", "fin",
+    "pOL0", "pOL1", "pOE", "c_d0", "c_d1", "c_x0", "c_x1", "c_s", "t1", "fin",
 ]
 
 
 def _bits(mask):
     return bin(mask).count("1")
+
+
+def _halves(mask):
+    e = [i for i in range(mask.bit_length()) if (mask >> i) & 1]
+    lo, hi = e[:len(e) // 2], e[len(e) // 2:]
+    return sum(1 << i for i in lo), sum(1 << i for i in hi)
 
 
 def rank_program(g, core, T, topo):
@@ -50,10 +57,17 @@ def rank_program(g, core, T, topo):
         m = topo.mask(core, dst)
         g.remote_dma(out_ap, in_ap, rsem, sem.lsem, pid, rid, m)
         sent[0] += _bits(m)
-        return _bits(m)
+
+    def xfer(dst, m, rsem, srcs, out_ap, op):
+        rid, pid = topo.addr(dst, core)
+        sent[0] += _bits(m)
+        return RemoteDMATransfer(dst_ids=[DstId(rid=rid, pnc=pid)], dma_engine_mask=m, remote_sem=rsem,
+                                 srcs=srcs, dsts=[out_ap], alu_op=op)
 
     n_off = _bits(topo.mask(core, X))
     n_on = _bits(topo.mask(core, sib))
+    m_lo, m_hi = _halves(topo.mask(core, X) & topo.mask(core, S))
+    n_half = _bits(m_lo)
 
     g.sync.dma_start(T.qd[:], T.q[:]).then_inc(sem.ld_qd, 16)
     g.scalar.dma_start(T.k0[:], T.k[:]).then_inc(sem.ld_k, 16)
@@ -62,15 +76,15 @@ def rank_program(g, core, T, topo):
     g.vector.memset(T.zeros[:], 0.0).then_inc(sem.z, 1)
 
     g.wait_ge(sem.ld_qd, 16)
-    send(X, T.qxd[:], T.qd[:], sem.a_qx)
-    send(S, T.qall[:, 1], T.qd[:], sem.a_qs)
+    g.remote_dma_fused([xfer(X, m_lo, sem.a_qx, [T.qd[:]], T.qxd[:], 0),
+                        xfer(S, m_hi, sem.a_qs, [T.qd[:]], T.qall[:, 1], 0)], local_sem=sem.lsem)
     g.wait_ge(sem.ld_k, 16)
     send(sib, T.k1[:], T.k0[:], sem.a_k)
     g.wait_ge(sem.ld_v, 16)
     send(sib, T.v1[:], T.v0[:], sem.a_v)
-    g.wait_ge(sem.a_qx, n_off)
+    g.wait_ge(sem.a_qx, n_half)
     send(S, T.qall[:, 3], T.qxd[:], sem.a_qd)
-    g.sync.wait_ge(sem.a_qx, n_off)
+    g.sync.wait_ge(sem.a_qx, n_half)
     g.sync.dma_start(T.qall[:, 2], T.qxd[:]).then_inc(sem.ld_qx, 16)
 
     te, ve = g.tensor, g.vector
@@ -80,6 +94,10 @@ def rank_program(g, core, T, topo):
     sL = (T.sL0, T.sL1, T.sL2, T.sL3)
     pL = (sem.pL0, sem.pL1, sem.pL2, sem.pL3)
     rL = (sem.rL0, sem.rL1, sem.rL2, sem.rL3)
+    psO = (T.psOL, T.psE0)
+    pOL = (sem.pOL0, sem.pOL1)
+    c_d, c_x = (sem.c_d0, sem.c_d1), (sem.c_x0, sem.c_x1)
+    a_raw, a_f = (sem.a_raw0, sem.a_raw1), (sem.a_f0, sem.a_f1)
 
     def hk(h):
         return slice(KP * h, KP * h + KP)
@@ -87,14 +105,24 @@ def rank_program(g, core, T, topo):
     def hq(h):
         return slice(QP * h, QP * h + QP)
 
+    def hs(b):
+        return slice(HH * b, HH * b + HH)
+
     te.wait_ge(sem.ld_q, 16)
-    te.wait_ge(sem.a_qs, n_off)
+    te.wait_ge(sem.a_qs, n_half)
     te.wait_ge(sem.ld_k, 16)
     for j in range(2):
         if j == 1:
             te.wait_ge(sem.a_k, n_on)
         for h in range(NH):
             te.matmul(psE[j][:, h], ks[j][:, hk(h)], T.qall[:, 0:2, hq(h)], True, True).then_inc(pE[j], 1)
+    te.wait_ge(sem.ld_v, 16)
+    te.wait_ge(sem.a_v, n_on)
+    te.wait_ge(sem.rE0, 1)
+    te.wait_ge(sem.rE1, 1)
+    for h in range(NH):
+        for j in range(2):
+            te.matmul(T.psOE[:, h], vs[j][:, hk(h)], sE[j][:, h], j == 0, j == 1).then_inc(sem.pOE, 1)
     te.wait_ge(sem.ld_qx, 16)
     te.wait_ge(sem.a_qd, n_off)
     for p in range(4):
@@ -102,51 +130,46 @@ def rank_program(g, core, T, topo):
             h = 2 * p + hh
             for j in range(2):
                 te.matmul(psL[p][:, 2 * hh + j], ks[j][:, hk(h)], T.qall[:, 2:4, hq(h)], True, True).then_inc(pL[p], 1)
-    te.wait_ge(sem.ld_v, 16)
-    te.wait_ge(sem.a_v, n_on)
     for p in range(4):
         te.wait_ge(rL[p], 1)
         for hh in range(2):
             h = 2 * p + hh
+            b = h // HH
             for j in range(2):
-                te.matmul(T.psOL[:, 0:2, hq(h)], vs[j][:, hk(h)], sL[p][:, 2 * hh + j], j == 0, j == 1).then_inc(sem.pOL, 1)
-    te.wait_ge(sem.rE0, 1)
-    te.wait_ge(sem.rE1, 1)
-    for h in range(NH):
-        for j in range(2):
-            te.matmul(T.psOE[:, 0:2, hq(h)], vs[j][:, hk(h)], sE[j][:, h], j == 0, j == 1).then_inc(sem.pOE, 1)
+                te.matmul(psO[b][:, h], vs[j][:, hk(h)], sL[p][:, 2 * hh + j], j == 0, j == 1).then_inc(pOL[b], 1)
 
     ve.wait_ge(sem.z, 1)
     for j in range(2):
         ve.wait_ge(pE[j], NH)
         ve.tensor_tensor(sE[j][:], psE[j][:], T.zeros[:], AluOpType.max).then_inc(rE[j], 1)
+    ve.wait_ge(sem.pOE, 2 * NH)
+    ve.tensor_copy(T.ob_s[:], T.psOE[:, :, 1]).then_inc(sem.c_s, 1)
     for p in range(4):
         ve.wait_ge(pL[p], 4)
         ve.tensor_tensor(sL[p][:], psL[p][:, 0:4], T.zeros[:, 0:4], AluOpType.max).then_inc(rL[p], 1)
-    ve.wait_ge(sem.pOL, 2 * NH)
-    ve.tensor_copy(T.ob_d[:], T.psOL[:, 1]).then_inc(sem.c_d, 1)
-    ve.tensor_copy(T.ob_x[:], T.psOL[:, 0]).then_inc(sem.c_x, 1)
-    ve.wait_ge(sem.pOE, 2 * NH)
-    ve.tensor_copy(T.ob_s[:], T.psOE[:, 1]).then_inc(sem.c_s, 1)
+    for b in range(2):
+        ve.wait_ge(pOL[b], 2 * HH)
+        ve.tensor_copy(T.ob_d[:, hs(b)], psO[b][:, hs(b), 1]).then_inc(c_d[b], 1)
+        ve.tensor_copy(T.ob_x[:, hs(b)], psO[b][:, hs(b), 0]).then_inc(c_x[b], 1)
     ve.wait_ge(sem.a_d, n_off)
-    ve.tensor_tensor(T.psOE[:, 0], T.psOE[:, 0], T.dland[:], AluOpType.add).then_inc(sem.t1, 1)
+    ve.tensor_tensor(T.psOE[:, :, 0], T.psOE[:, :, 0], T.dland[:], AluOpType.add).then_inc(sem.t1, 1)
     ve.wait_ge(sem.t1, 1)
-    ve.wait_ge(sem.a_f, n_off)
-    ve.tensor_tensor(T.ybuf[:], T.psOE[:, 0], T.fland[:], AluOpType.add).then_inc(sem.fin, 1)
+    for b in range(2):
+        ve.wait_ge(a_f[b], n_off)
+        ve.tensor_tensor(T.ybuf[:, hs(b)], T.psOE[:, hs(b), 0], T.fland[:, hs(b)], AluOpType.add).then_inc(sem.fin, 1)
 
-    g.wait_ge(sem.c_d, 1)
-    send(S, T.rawland[:], T.ob_d[:], sem.a_raw)
     g.wait_ge(sem.c_s, 1)
     send(S, T.dland[:], T.ob_s[:], sem.a_d)
-    g.wait_ge(sem.c_x, 1)
-    g.wait_ge(sem.a_raw, n_off)
-    rid, pid = topo.addr(X, core)
-    g.remote_dma_fused([RemoteDMATransfer(dst_ids=[DstId(rid=rid, pnc=pid)], dma_engine_mask=topo.mask(core, X),
-                                          remote_sem=sem.a_f, srcs=[T.rawland[:], T.ob_x[:]], dsts=[T.fland[:]],
-                                          alu_op=1)], local_sem=sem.lsem)
-    sent[0] += n_off
+    for b in range(2):
+        g.wait_ge(c_d[b], 1)
+        send(S, T.rawland[:, hs(b)], T.ob_d[:, hs(b)], a_raw[b])
+    for b in range(2):
+        g.wait_ge(c_x[b], 1)
+        g.wait_ge(a_raw[b], n_off)
+        g.remote_dma_fused([xfer(X, topo.mask(core, X), a_f[b], [T.rawland[:, hs(b)], T.ob_x[:, hs(b)]],
+                                 T.fland[:, hs(b)], 1)], local_sem=sem.lsem)
 
-    g.sync.wait_ge(sem.fin, 1)
+    g.sync.wait_ge(sem.fin, 2)
     g.sync.dma_start(T.y[:], T.ybuf[:]).then_inc(sem.st_y, 16)
     g.sync.wait_ge(sem.st_y, 16)
     g.wait_ge(sem.lsem, sent[0])

@@ -2,34 +2,38 @@ from concourse.bass import DstId, RemoteDMATransfer
 from concourse.mybir import AluOpType
 
 NH, QP, KP = 8, 32, 128
-W = NH * QP
 HH = NH // 2
+WH = HH * QP
+KH = HH * KP
 BF, F32 = "bfloat16", "float32"
 
 SCRATCH = {
-    "qall": ("sbuf", [128, 4, W], BF),
+    "ql": ("sbuf", [128, 4, WH], BF),
     "k0": ("sbuf", [128, NH * KP], BF), "v0": ("sbuf", [128, NH * KP], BF),
-    "k1": ("sbuf", [128, NH * KP], BF), "v1": ("sbuf", [128, NH * KP], BF),
-    "zeros": ("sbuf", [128, NH, 2, QP], F32),
-    "sE0": ("sbuf", [128, NH, 2, QP], BF), "sE1": ("sbuf", [128, NH, 2, QP], BF),
-    "sL0": ("sbuf", [128, 4, 2, QP], BF), "sL1": ("sbuf", [128, 4, 2, QP], BF),
-    "sL2": ("sbuf", [128, 4, 2, QP], BF), "sL3": ("sbuf", [128, 4, 2, QP], BF),
-    "ob_s": ("sbuf", [128, NH, QP], BF), "ob_x": ("sbuf", [128, NH, QP], BF), "ob_d": ("sbuf", [128, NH, QP], BF),
-    "rawland": ("sbuf", [128, NH, QP], BF), "dland": ("sbuf", [128, NH, QP], BF), "fland": ("sbuf", [128, NH, QP], BF),
+    "ka": ("sbuf", [128, KH], BF), "va": ("sbuf", [128, KH], BF),
+    "kb": ("sbuf", [128, KH], BF), "vb": ("sbuf", [128, KH], BF),
+    "zeros": ("sbuf", [128, HH, 2, QP], F32),
+    "sE0": ("sbuf", [128, HH, 2, QP], BF), "sE1": ("sbuf", [128, HH, 2, QP], BF),
+    "sL": ("sbuf", [128, HH, 2, 2, QP], BF),
+    "ob_s": ("sbuf", [128, HH, QP], BF), "ob_x": ("sbuf", [128, HH, QP], BF), "ob_d": ("sbuf", [128, HH, QP], BF),
+    "ob_o": ("sbuf", [128, HH, QP], BF),
+    "rawland": ("sbuf", [128, HH, QP], BF),
+    "dland": ("sbuf", [128, NH, QP], BF), "fland": ("sbuf", [128, NH, QP], BF), "oland": ("sbuf", [128, HH, QP], BF),
+    "acc": ("sbuf", [128, HH, QP], F32),
     "ybuf": ("sbuf", [128, NH, QP], BF),
-    "qd": ("dram", [128, W], BF),
-    "qxd": ("dram", [128, W], BF),
+    "qd": ("dram", [2, 128, WH], BF),
+    "qxd": ("dram", [2, 128, WH], BF),
     "psE0": ("psum", [128, NH, 2, QP], F32), "psE1": ("psum", [128, NH, 2, QP], F32),
     "psL0": ("psum", [128, NH, 2, QP], F32), "psL1": ("psum", [128, NH, 2, QP], F32),
     "psL2": ("psum", [128, NH, 2, QP], F32), "psL3": ("psum", [128, NH, 2, QP], F32),
     "psOL": ("psum", [128, NH, 2, QP], F32), "psOE": ("psum", [128, NH, 2, QP], F32),
 }
 SEMAPHORES = [
-    "ld_qd", "ld_q", "ld_k", "ld_v", "ld_qx", "st_y",
-    "a_qx", "a_qs", "a_qd", "a_k", "a_v", "a_raw0", "a_raw1", "a_d", "a_f0", "a_f1", "lsem", "z",
-    "pE0", "pE1", "rE0", "rE1", "pL0", "pL1", "pL2", "pL3", "rL0", "rL1", "rL2", "rL3",
-    "pOL0", "pOL1", "pOE", "c_d0", "c_d1", "c_x0", "c_x1", "c_s", "t1", "fin",
-]
+    "ld_qd0", "ld_qd1", "ld_q", "ld_k", "ld_v", "ld_qx", "st_y0", "st_y1",
+    "a_qx0", "a_qx1", "a_qs", "a_qo", "a_qxh", "a_qd", "a_ka", "a_kb", "a_va", "a_vb",
+    "a_raw", "a_d0", "a_d1", "a_o", "a_f0", "a_f1", "lsem", "z",
+    "pE0", "pE1", "rE0", "rE1", "pOL", "pOE", "c_d", "c_x", "c_s", "c_o", "t1", "t2", "fin0", "fin1",
+] + ["pL%d" % h for h in range(HH)] + ["rL%d" % h for h in range(HH)]
 
 
 def _bits(mask):
@@ -42,62 +46,47 @@ def _halves(mask):
     return sum(1 << i for i in lo), sum(1 << i for i in hi)
 
 
+def _helper(rc, T, topo):
+    c = [x for x in range(max(rc - 16, 0), rc + 17)
+         if topo.host(x) == topo.host(rc) and topo.chip(x) == topo.chip(rc) and topo.die(x) == topo.die(rc)
+         and T.rank_of(x) is None]
+    return max(c, key=lambda x: abs(x - rc))
+
+
 def rank_program(g, core, T, topo):
-    if T.rank_of(core) is None:
-        return
+    helper = {rc: _helper(rc, T, topo) for rc in T.cores}
+    is_rank = T.rank_of(core) is not None
+    if is_rank:
+        rc = core
+    else:
+        own = [r for r in T.cores if helper[r] == core]
+        if not own:
+            return
+        rc = own[0]
+    lane = 0 if is_rank else 1
     sem = T.sem
-    sib = [c for c in T.cores if c != core and topo.host(c) == topo.host(core) and topo.chip(c) == topo.chip(core)][0]
-    far = [c for c in T.cores if topo.host(c) != topo.host(core) and topo.die(c) == topo.die(core)]
-    S = [c for c in far if topo.same_plane(core, c)][0]
-    X = [c for c in far if topo.may_write(core, c) and not topo.same_plane(core, c)][0]
+    sib = [c for c in T.cores if c != rc and topo.host(c) == topo.host(rc) and topo.chip(c) == topo.chip(rc)][0]
+    far = [c for c in T.cores if topo.host(c) != topo.host(rc) and topo.die(c) == topo.die(rc)]
+    S = [c for c in far if topo.same_plane(rc, c)][0]
+    X = [c for c in far if topo.may_write(rc, c) and not topo.same_plane(rc, c)][0]
+    S_lane = S if is_rank else helper[S]
     sent = [0]
 
-    def send(dst, out_ap, in_ap, rsem):
-        rid, pid = topo.addr(dst, core)
-        m = topo.mask(core, dst)
-        g.remote_dma(out_ap, in_ap, rsem, sem.lsem, pid, rid, m)
-        sent[0] += _bits(m)
-
-    def xfer(dst, m, rsem, srcs, out_ap, op):
+    def xfer(dst, m, rsem, srcs, out_ap, op=0):
         rid, pid = topo.addr(dst, core)
         sent[0] += _bits(m)
         return RemoteDMATransfer(dst_ids=[DstId(rid=rid, pnc=pid)], dma_engine_mask=m, remote_sem=rsem,
                                  srcs=srcs, dsts=[out_ap], alu_op=op)
 
-    n_off = _bits(topo.mask(core, X))
-    n_on = _bits(topo.mask(core, sib))
-    m_lo, m_hi = _halves(topo.mask(core, X) & topo.mask(core, S))
-    n_half = _bits(m_lo)
+    def call(*xs):
+        g.remote_dma_fused(list(xs), local_sem=sem.lsem)
 
-    g.sync.dma_start(T.qd[:], T.q[:]).then_inc(sem.ld_qd, 16)
-    g.scalar.dma_start(T.k0[:], T.k[:]).then_inc(sem.ld_k, 16)
-    g.sync.dma_start(T.qall[:, 0], T.q[:]).then_inc(sem.ld_q, 16)
-    g.sync.dma_start(T.v0[:], T.v[:]).then_inc(sem.ld_v, 16)
-    g.vector.memset(T.zeros[:], 0.0).then_inc(sem.z, 1)
-
-    g.wait_ge(sem.ld_qd, 16)
-    g.remote_dma_fused([xfer(X, m_lo, sem.a_qx, [T.qd[:]], T.qxd[:], 0),
-                        xfer(S, m_hi, sem.a_qs, [T.qd[:]], T.qall[:, 1], 0)], local_sem=sem.lsem)
-    g.wait_ge(sem.ld_k, 16)
-    send(sib, T.k1[:], T.k0[:], sem.a_k)
-    g.wait_ge(sem.ld_v, 16)
-    send(sib, T.v1[:], T.v0[:], sem.a_v)
-    g.wait_ge(sem.a_qx, n_half)
-    send(S, T.qall[:, 3], T.qxd[:], sem.a_qd)
-    g.sync.wait_ge(sem.a_qx, n_half)
-    g.sync.dma_start(T.qall[:, 2], T.qxd[:]).then_inc(sem.ld_qx, 16)
-
-    te, ve = g.tensor, g.vector
-    ks, vs = (T.k0, T.k1), (T.v0, T.v1)
-    psE, sE, pE, rE = (T.psE0, T.psE1), (T.sE0, T.sE1), (sem.pE0, sem.pE1), (sem.rE0, sem.rE1)
-    psL = (T.psL0, T.psL1, T.psL2, T.psL3)
-    sL = (T.sL0, T.sL1, T.sL2, T.sL3)
-    pL = (sem.pL0, sem.pL1, sem.pL2, sem.pL3)
-    rL = (sem.rL0, sem.rL1, sem.rL2, sem.rL3)
-    psO = (T.psOL, T.psE0)
-    pOL = (sem.pOL0, sem.pOL1)
-    c_d, c_x = (sem.c_d0, sem.c_d1), (sem.c_x0, sem.c_x1)
-    a_raw, a_f = (sem.a_raw0, sem.a_raw1), (sem.a_f0, sem.a_f1)
+    m_off = topo.mask(core, X) & topo.mask(core, S)
+    m_chip = topo.mask(core, sib) & ~m_off
+    m_lo, m_hi = _halves(m_off)
+    m_hi0, m_hi1 = _halves(m_hi)
+    m_c0, m_c1 = _halves(m_chip)
+    n_off, n_chip, n_half, n_q, n_c = _bits(m_off), _bits(m_chip), _bits(m_lo), _bits(m_hi0), _bits(m_c0)
 
     def hk(h):
         return slice(KP * h, KP * h + KP)
@@ -108,68 +97,127 @@ def rank_program(g, core, T, topo):
     def hs(b):
         return slice(HH * b, HH * b + HH)
 
-    te.wait_ge(sem.ld_q, 16)
-    te.wait_ge(sem.a_qs, n_half)
-    te.wait_ge(sem.ld_k, 16)
+    def hw(b):
+        return slice(WH * b, WH * b + WH)
+
+    g.vector.memset(T.zeros[:], 0.0).then_inc(sem.z, 1)
+
+    if is_rank:
+        hlp, hsib = helper[rc], helper[sib]
+        ld_qd, a_qx = (sem.ld_qd0, sem.ld_qd1), (sem.a_qx0, sem.a_qx1)
+        g.sync.dma_start(T.qd[0], T.q[:, hw(0)]).then_inc(ld_qd[0], 16)
+        g.scalar.dma_start(T.qd[1], T.q[:, hw(1)]).then_inc(ld_qd[1], 16)
+        g.scalar.dma_start(T.k0[:], T.k[:]).then_inc(sem.ld_k, 16)
+        g.sync.dma_start(T.ql[:, 0], T.q[:, hw(0)]).then_inc(sem.ld_q, 16)
+        g.sync.dma_start(T.v0[:], T.v[:]).then_inc(sem.ld_v, 16)
+        for b in range(2):
+            g.wait_ge(ld_qd[b], 16)
+            call(xfer(X, m_lo, a_qx[b], [T.qd[b]], T.qxd[b]))
+        call(xfer(S, m_hi0, sem.a_qs, [T.qd[0]], T.ql[:, 1]),
+             xfer(helper[S], m_hi1, sem.a_qs, [T.qd[1]], T.ql[:, 1]),
+             xfer(hlp, m_c0, sem.a_qo, [T.qd[1]], T.ql[:, 0]))
+        g.wait_ge(sem.ld_k, 16)
+        call(xfer(sib, m_off, sem.a_kb, [T.k0[:, 0:KH]], T.kb[:]),
+             xfer(hlp, m_c0, sem.a_ka, [T.k0[:, KH:2 * KH]], T.ka[:]),
+             xfer(hsib, m_c1, sem.a_kb, [T.k0[:, KH:2 * KH]], T.kb[:]))
+        g.wait_ge(sem.ld_v, 16)
+        call(xfer(sib, m_off, sem.a_vb, [T.v0[:, 0:KH]], T.vb[:]),
+             xfer(hlp, m_c0, sem.a_va, [T.v0[:, KH:2 * KH]], T.va[:]),
+             xfer(hsib, m_c1, sem.a_vb, [T.v0[:, KH:2 * KH]], T.vb[:]))
+        g.wait_ge(a_qx[0], n_half)
+        call(xfer(S, m_off, sem.a_qd, [T.qxd[0]], T.ql[:, 3]))
+        g.sync.wait_ge(a_qx[0], n_half)
+        g.sync.dma_start(T.ql[:, 2], T.qxd[0]).then_inc(sem.ld_qx, 16)
+        g.wait_ge(a_qx[1], n_half)
+        call(xfer(helper[S], m_off, sem.a_qd, [T.qxd[1]], T.ql[:, 3]),
+             xfer(hlp, m_chip, sem.a_qxh, [T.qxd[1]], T.ql[:, 2]))
+
+    te, ve = g.tensor, g.vector
+    ks, vs = ((T.k0, T.kb), (T.v0, T.vb)) if is_rank else ((T.ka, T.kb), (T.va, T.vb))
+    n_b = n_off if is_rank else n_c
+    psE, sE, pE, rE = (T.psE0, T.psE1), (T.sE0, T.sE1), (sem.pE0, sem.pE1), (sem.rE0, sem.rE1)
+    psL = (T.psL0, T.psL1, T.psL2, T.psL3)
+    pL = [sem["pL%d" % h] for h in range(HH)]
+    rL = [sem["rL%d" % h] for h in range(HH)]
+
+    if is_rank:
+        te.wait_ge(sem.ld_q, 16)
+        te.wait_ge(sem.ld_k, 16)
+    else:
+        te.wait_ge(sem.a_qo, n_c)
+        te.wait_ge(sem.a_ka, n_c)
+    te.wait_ge(sem.a_qs, n_q)
     for j in range(2):
         if j == 1:
-            te.wait_ge(sem.a_k, n_on)
-        for h in range(NH):
-            te.matmul(psE[j][:, h], ks[j][:, hk(h)], T.qall[:, 0:2, hq(h)], True, True).then_inc(pE[j], 1)
-    te.wait_ge(sem.ld_v, 16)
-    te.wait_ge(sem.a_v, n_on)
+            te.wait_ge(sem.a_kb, n_b)
+        for h in range(HH):
+            te.matmul(psE[j][:, h], ks[j][:, hk(h)], T.ql[:, 0:2, hq(h)], True, True).then_inc(pE[j], 1)
+    if is_rank:
+        te.wait_ge(sem.ld_v, 16)
+    else:
+        te.wait_ge(sem.a_va, n_c)
+    te.wait_ge(sem.a_vb, n_b)
     te.wait_ge(sem.rE0, 1)
     te.wait_ge(sem.rE1, 1)
-    for h in range(NH):
+    for h in range(HH):
         for j in range(2):
             te.matmul(T.psOE[:, h], vs[j][:, hk(h)], sE[j][:, h], j == 0, j == 1).then_inc(sem.pOE, 1)
-    te.wait_ge(sem.ld_qx, 16)
+    if is_rank:
+        te.wait_ge(sem.ld_qx, 16)
+    else:
+        te.wait_ge(sem.a_qxh, n_chip)
     te.wait_ge(sem.a_qd, n_off)
-    for p in range(4):
-        for hh in range(2):
-            h = 2 * p + hh
-            for j in range(2):
-                te.matmul(psL[p][:, 2 * hh + j], ks[j][:, hk(h)], T.qall[:, 2:4, hq(h)], True, True).then_inc(pL[p], 1)
-    for p in range(4):
-        te.wait_ge(rL[p], 1)
-        for hh in range(2):
-            h = 2 * p + hh
-            b = h // HH
-            for j in range(2):
-                te.matmul(psO[b][:, h], vs[j][:, hk(h)], sL[p][:, 2 * hh + j], j == 0, j == 1).then_inc(pOL[b], 1)
+    for h in range(HH):
+        for j in range(2):
+            te.matmul(psL[h][:, j], ks[j][:, hk(h)], T.ql[:, 2:4, hq(h)], True, True).then_inc(pL[h], 1)
+    for h in range(HH):
+        te.wait_ge(rL[h], 1)
+        for j in range(2):
+            te.matmul(T.psOL[:, h], vs[j][:, hk(h)], T.sL[:, h, j], j == 0, j == 1).then_inc(sem.pOL, 1)
 
     ve.wait_ge(sem.z, 1)
     for j in range(2):
-        ve.wait_ge(pE[j], NH)
-        ve.tensor_tensor(sE[j][:], psE[j][:], T.zeros[:], AluOpType.max).then_inc(rE[j], 1)
-    ve.wait_ge(sem.pOE, 2 * NH)
-    ve.tensor_copy(T.ob_s[:], T.psOE[:, :, 1]).then_inc(sem.c_s, 1)
-    for p in range(4):
-        ve.wait_ge(pL[p], 4)
-        ve.tensor_tensor(sL[p][:], psL[p][:, 0:4], T.zeros[:, 0:4], AluOpType.max).then_inc(rL[p], 1)
-    for b in range(2):
-        ve.wait_ge(pOL[b], 2 * HH)
-        ve.tensor_copy(T.ob_d[:, hs(b)], psO[b][:, hs(b), 1]).then_inc(c_d[b], 1)
-        ve.tensor_copy(T.ob_x[:, hs(b)], psO[b][:, hs(b), 0]).then_inc(c_x[b], 1)
-    ve.wait_ge(sem.a_d, n_off)
-    ve.tensor_tensor(T.psOE[:, :, 0], T.psOE[:, :, 0], T.dland[:], AluOpType.add).then_inc(sem.t1, 1)
-    ve.wait_ge(sem.t1, 1)
-    for b in range(2):
-        ve.wait_ge(a_f[b], n_off)
-        ve.tensor_tensor(T.ybuf[:, hs(b)], T.psOE[:, hs(b), 0], T.fland[:, hs(b)], AluOpType.add).then_inc(sem.fin, 1)
+        ve.wait_ge(pE[j], HH)
+        ve.tensor_tensor(sE[j][:], psE[j][:, 0:HH], T.zeros[:], AluOpType.max).then_inc(rE[j], 1)
+    ve.wait_ge(sem.pOE, 2 * HH)
+    ve.tensor_copy(T.ob_s[:], T.psOE[:, 0:HH, 1]).then_inc(sem.c_s, 1)
+    if not is_rank:
+        ve.tensor_copy(T.ob_o[:], T.psOE[:, 0:HH, 0]).then_inc(sem.c_o, 1)
+    for h in range(HH):
+        ve.wait_ge(pL[h], 2)
+        ve.tensor_tensor(T.sL[:, h], psL[h][:, 0:2], T.zeros[:, 0:2], AluOpType.max).then_inc(rL[h], 1)
+    ve.wait_ge(sem.pOL, 2 * HH)
+    ve.tensor_copy(T.ob_d[:], T.psOL[:, 0:HH, 1]).then_inc(sem.c_d, 1)
+    ve.tensor_copy(T.ob_x[:], T.psOL[:, 0:HH, 0]).then_inc(sem.c_x, 1)
+    if is_rank:
+        ve.wait_ge(sem.a_d0, n_off)
+        ve.tensor_tensor(T.psOE[:, 0:HH, 0], T.psOE[:, 0:HH, 0], T.dland[:, hs(0)], AluOpType.add).then_inc(sem.t1, 1)
+        ve.wait_ge(sem.a_o, n_c)
+        ve.wait_ge(sem.a_d1, n_off)
+        ve.tensor_tensor(T.acc[:], T.oland[:], T.dland[:, hs(1)], AluOpType.add).then_inc(sem.t2, 1)
+        ve.wait_ge(sem.t1, 1)
+        ve.wait_ge(sem.a_f0, n_off)
+        ve.tensor_tensor(T.ybuf[:, hs(0)], T.psOE[:, 0:HH, 0], T.fland[:, hs(0)], AluOpType.add).then_inc(sem.fin0, 1)
+        ve.wait_ge(sem.t2, 1)
+        ve.wait_ge(sem.a_f1, n_off)
+        ve.tensor_tensor(T.ybuf[:, hs(1)], T.acc[:], T.fland[:, hs(1)], AluOpType.add).then_inc(sem.fin1, 1)
 
     g.wait_ge(sem.c_s, 1)
-    send(S, T.dland[:], T.ob_s[:], sem.a_d)
-    for b in range(2):
-        g.wait_ge(c_d[b], 1)
-        send(S, T.rawland[:, hs(b)], T.ob_d[:, hs(b)], a_raw[b])
-    for b in range(2):
-        g.wait_ge(c_x[b], 1)
-        g.wait_ge(a_raw[b], n_off)
-        g.remote_dma_fused([xfer(X, topo.mask(core, X), a_f[b], [T.rawland[:, hs(b)], T.ob_x[:, hs(b)]],
-                                 T.fland[:, hs(b)], 1)], local_sem=sem.lsem)
+    if is_rank:
+        call(xfer(S, m_off, sem.a_d0, [T.ob_s[:]], T.dland[:, hs(0)]))
+    else:
+        g.wait_ge(sem.c_o, 1)
+        call(xfer(S, m_off, sem.a_d1, [T.ob_s[:]], T.dland[:, hs(1)]),
+             xfer(rc, m_c0, sem.a_o, [T.ob_o[:]], T.oland[:]))
+    g.wait_ge(sem.c_d, 1)
+    call(xfer(S_lane, m_off, sem.a_raw, [T.ob_d[:]], T.rawland[:]))
+    g.wait_ge(sem.c_x, 1)
+    g.wait_ge(sem.a_raw, n_off)
+    call(xfer(X, m_off, sem.a_f1 if lane else sem.a_f0, [T.rawland[:], T.ob_x[:]], T.fland[:, hs(lane)], 1))
 
-    g.sync.wait_ge(sem.fin, 2)
-    g.sync.dma_start(T.y[:], T.ybuf[:]).then_inc(sem.st_y, 16)
-    g.sync.wait_ge(sem.st_y, 16)
+    if is_rank:
+        for b, qu, f, st in ((0, g.sync, sem.fin0, sem.st_y0), (1, g.scalar, sem.fin1, sem.st_y1)):
+            qu.wait_ge(f, 1)
+            qu.dma_start(T.y[:, hw(b)], T.ybuf[:, hs(b)]).then_inc(st, 16)
+            qu.wait_ge(st, 16)
     g.wait_ge(sem.lsem, sent[0])

from concourse.bass import DstId, RemoteDMATransfer
from concourse.mybir import AluOpType

NH, QP, KP = 8, 32, 128
HH = NH // 2
WH = HH * QP
KH = HH * KP
BF, F32 = "bfloat16", "float32"

SCRATCH = {
    "ql": ("sbuf", [128, 4, WH], BF),
    "k0": ("sbuf", [128, NH * KP], BF), "v0": ("sbuf", [128, NH * KP], BF),
    "ka": ("sbuf", [128, KH], BF), "va": ("sbuf", [128, KH], BF),
    "kb": ("sbuf", [128, KH], BF), "vb": ("sbuf", [128, KH], BF),
    "zeros": ("sbuf", [128, HH, 2, QP], F32),
    "sE0": ("sbuf", [128, HH, 2, QP], BF), "sE1": ("sbuf", [128, HH, 2, QP], BF),
    "sL": ("sbuf", [128, HH, 2, 2, QP], BF),
    "ob_s": ("sbuf", [128, HH, QP], BF), "ob_x": ("sbuf", [128, HH, QP], BF), "ob_d": ("sbuf", [128, HH, QP], BF),
    "ob_o": ("sbuf", [128, HH, QP], BF),
    "rawland": ("sbuf", [128, HH, QP], BF),
    "dland": ("sbuf", [128, NH, QP], BF), "fland": ("sbuf", [128, NH, QP], BF), "oland": ("sbuf", [128, HH, QP], BF),
    "acc": ("sbuf", [128, HH, QP], F32),
    "ybuf": ("sbuf", [128, NH, QP], BF),
    "qd": ("dram", [2, 128, WH], BF),
    "qxd": ("dram", [2, 128, WH], BF),
    "psE0": ("psum", [128, NH, 2, QP], F32), "psE1": ("psum", [128, NH, 2, QP], F32),
    "psL0": ("psum", [128, NH, 2, QP], F32), "psL1": ("psum", [128, NH, 2, QP], F32),
    "psL2": ("psum", [128, NH, 2, QP], F32), "psL3": ("psum", [128, NH, 2, QP], F32),
    "psOL": ("psum", [128, NH, 2, QP], F32), "psOE": ("psum", [128, NH, 2, QP], F32),
}
SEMAPHORES = [
    "ld_qd0", "ld_qd1", "ld_q", "ld_k", "ld_v", "ld_qx", "st_y0", "st_y1",
    "a_qx0", "a_qx1", "a_qs", "a_qo", "a_qxh", "a_qd", "a_ka", "a_kb", "a_va", "a_vb",
    "a_raw", "a_d0", "a_d1", "a_o", "a_f0", "a_f1", "lsem", "z",
    "pE0", "pE1", "rE0", "rE1", "pOL", "pOE", "c_d", "c_x", "c_s", "c_o", "t1", "t2", "fin0", "fin1",
] + ["pL%d" % h for h in range(HH)] + ["rL%d" % h for h in range(HH)]


def _bits(mask):
    return bin(mask).count("1")


def _halves(mask):
    e = [i for i in range(mask.bit_length()) if (mask >> i) & 1]
    lo, hi = e[:len(e) // 2], e[len(e) // 2:]
    return sum(1 << i for i in lo), sum(1 << i for i in hi)


def _helper(rc, T, topo):
    c = [x for x in range(max(rc - 16, 0), rc + 17)
         if topo.host(x) == topo.host(rc) and topo.chip(x) == topo.chip(rc) and topo.die(x) == topo.die(rc)
         and T.rank_of(x) is None]
    return max(c, key=lambda x: abs(x - rc))


def rank_program(g, core, T, topo):
    helper = {rc: _helper(rc, T, topo) for rc in T.cores}
    is_rank = T.rank_of(core) is not None
    if is_rank:
        rc = core
    else:
        own = [r for r in T.cores if helper[r] == core]
        if not own:
            return
        rc = own[0]
    lane = 0 if is_rank else 1
    sem = T.sem
    sib = [c for c in T.cores if c != rc and topo.host(c) == topo.host(rc) and topo.chip(c) == topo.chip(rc)][0]
    far = [c for c in T.cores if topo.host(c) != topo.host(rc) and topo.die(c) == topo.die(rc)]
    S = [c for c in far if topo.same_plane(rc, c)][0]
    X = [c for c in far if topo.may_write(rc, c) and not topo.same_plane(rc, c)][0]
    S_lane = S if is_rank else helper[S]
    sent = [0]

    def xfer(dst, m, rsem, srcs, out_ap, op=0):
        rid, pid = topo.addr(dst, core)
        sent[0] += _bits(m)
        return RemoteDMATransfer(dst_ids=[DstId(rid=rid, pnc=pid)], dma_engine_mask=m, remote_sem=rsem,
                                 srcs=srcs, dsts=[out_ap], alu_op=op)

    def call(*xs):
        g.remote_dma_fused(list(xs), local_sem=sem.lsem)

    m_off = topo.mask(core, X) & topo.mask(core, S)
    m_chip = topo.mask(core, sib) & ~m_off
    m_lo, m_hi = _halves(m_off)
    m_hi0, m_hi1 = _halves(m_hi)
    m_c0, m_c1 = _halves(m_chip)
    n_off, n_chip, n_half, n_q, n_c = _bits(m_off), _bits(m_chip), _bits(m_lo), _bits(m_hi0), _bits(m_c0)

    def hk(h):
        return slice(KP * h, KP * h + KP)

    def hq(h):
        return slice(QP * h, QP * h + QP)

    def hs(b):
        return slice(HH * b, HH * b + HH)

    def hw(b):
        return slice(WH * b, WH * b + WH)

    g.vector.memset(T.zeros[:], 0.0).then_inc(sem.z, 1)

    if is_rank:
        hlp, hsib = helper[rc], helper[sib]
        ld_qd, a_qx = (sem.ld_qd0, sem.ld_qd1), (sem.a_qx0, sem.a_qx1)
        g.sync.dma_start(T.qd[0], T.q[:, hw(0)]).then_inc(ld_qd[0], 16)
        g.scalar.dma_start(T.qd[1], T.q[:, hw(1)]).then_inc(ld_qd[1], 16)
        g.scalar.dma_start(T.k0[:], T.k[:]).then_inc(sem.ld_k, 16)
        g.sync.dma_start(T.ql[:, 0], T.q[:, hw(0)]).then_inc(sem.ld_q, 16)
        g.sync.dma_start(T.v0[:], T.v[:]).then_inc(sem.ld_v, 16)
        for b in range(2):
            g.wait_ge(ld_qd[b], 16)
            call(xfer(X, m_lo, a_qx[b], [T.qd[b]], T.qxd[b]))
        call(xfer(S, m_hi0, sem.a_qs, [T.qd[0]], T.ql[:, 1]),
             xfer(helper[S], m_hi1, sem.a_qs, [T.qd[1]], T.ql[:, 1]),
             xfer(hlp, m_c0, sem.a_qo, [T.qd[1]], T.ql[:, 0]))
        g.wait_ge(sem.ld_k, 16)
        call(xfer(sib, m_off, sem.a_kb, [T.k0[:, 0:KH]], T.kb[:]),
             xfer(hlp, m_c0, sem.a_ka, [T.k0[:, KH:2 * KH]], T.ka[:]),
             xfer(hsib, m_c1, sem.a_kb, [T.k0[:, KH:2 * KH]], T.kb[:]))
        g.wait_ge(sem.ld_v, 16)
        call(xfer(sib, m_off, sem.a_vb, [T.v0[:, 0:KH]], T.vb[:]),
             xfer(hlp, m_c0, sem.a_va, [T.v0[:, KH:2 * KH]], T.va[:]),
             xfer(hsib, m_c1, sem.a_vb, [T.v0[:, KH:2 * KH]], T.vb[:]))
        g.wait_ge(a_qx[0], n_half)
        call(xfer(S, m_off, sem.a_qd, [T.qxd[0]], T.ql[:, 3]))
        g.sync.wait_ge(a_qx[0], n_half)
        g.sync.dma_start(T.ql[:, 2], T.qxd[0]).then_inc(sem.ld_qx, 16)
        g.wait_ge(a_qx[1], n_half)
        call(xfer(helper[S], m_off, sem.a_qd, [T.qxd[1]], T.ql[:, 3]),
             xfer(hlp, m_chip, sem.a_qxh, [T.qxd[1]], T.ql[:, 2]))

    te, ve = g.tensor, g.vector
    ks, vs = ((T.k0, T.kb), (T.v0, T.vb)) if is_rank else ((T.ka, T.kb), (T.va, T.vb))
    n_b = n_off if is_rank else n_c
    psE, sE, pE, rE = (T.psE0, T.psE1), (T.sE0, T.sE1), (sem.pE0, sem.pE1), (sem.rE0, sem.rE1)
    psL = (T.psL0, T.psL1, T.psL2, T.psL3)
    pL = [sem["pL%d" % h] for h in range(HH)]
    rL = [sem["rL%d" % h] for h in range(HH)]

    if is_rank:
        te.wait_ge(sem.ld_q, 16)
        te.wait_ge(sem.ld_k, 16)
    else:
        te.wait_ge(sem.a_qo, n_c)
        te.wait_ge(sem.a_ka, n_c)
    te.wait_ge(sem.a_qs, n_q)
    for j in range(2):
        if j == 1:
            te.wait_ge(sem.a_kb, n_b)
        for h in range(HH):
            te.matmul(psE[j][:, h], ks[j][:, hk(h)], T.ql[:, 0:2, hq(h)], True, True).then_inc(pE[j], 1)
    if is_rank:
        te.wait_ge(sem.ld_v, 16)
    else:
        te.wait_ge(sem.a_va, n_c)
    te.wait_ge(sem.a_vb, n_b)
    te.wait_ge(sem.rE0, 1)
    te.wait_ge(sem.rE1, 1)
    for h in range(HH):
        for j in range(2):
            te.matmul(T.psOE[:, h], vs[j][:, hk(h)], sE[j][:, h], j == 0, j == 1).then_inc(sem.pOE, 1)
    if is_rank:
        te.wait_ge(sem.ld_qx, 16)
    else:
        te.wait_ge(sem.a_qxh, n_chip)
    te.wait_ge(sem.a_qd, n_off)
    for h in range(HH):
        for j in range(2):
            te.matmul(psL[h][:, j], ks[j][:, hk(h)], T.ql[:, 2:4, hq(h)], True, True).then_inc(pL[h], 1)
    for h in range(HH):
        te.wait_ge(rL[h], 1)
        for j in range(2):
            te.matmul(T.psOL[:, h], vs[j][:, hk(h)], T.sL[:, h, j], j == 0, j == 1).then_inc(sem.pOL, 1)

    ve.wait_ge(sem.z, 1)
    for j in range(2):
        ve.wait_ge(pE[j], HH)
        ve.tensor_tensor(sE[j][:], psE[j][:, 0:HH], T.zeros[:], AluOpType.max).then_inc(rE[j], 1)
    ve.wait_ge(sem.pOE, 2 * HH)
    ve.tensor_copy(T.ob_s[:], T.psOE[:, 0:HH, 1]).then_inc(sem.c_s, 1)
    if not is_rank:
        ve.tensor_copy(T.ob_o[:], T.psOE[:, 0:HH, 0]).then_inc(sem.c_o, 1)
    for h in range(HH):
        ve.wait_ge(pL[h], 2)
        ve.tensor_tensor(T.sL[:, h], psL[h][:, 0:2], T.zeros[:, 0:2], AluOpType.max).then_inc(rL[h], 1)
    ve.wait_ge(sem.pOL, 2 * HH)
    ve.tensor_copy(T.ob_d[:], T.psOL[:, 0:HH, 1]).then_inc(sem.c_d, 1)
    ve.tensor_copy(T.ob_x[:], T.psOL[:, 0:HH, 0]).then_inc(sem.c_x, 1)
    if is_rank:
        ve.wait_ge(sem.a_d0, n_off)
        ve.tensor_tensor(T.psOE[:, 0:HH, 0], T.psOE[:, 0:HH, 0], T.dland[:, hs(0)], AluOpType.add).then_inc(sem.t1, 1)
        ve.wait_ge(sem.a_o, n_c)
        ve.wait_ge(sem.a_d1, n_off)
        ve.tensor_tensor(T.acc[:], T.oland[:], T.dland[:, hs(1)], AluOpType.add).then_inc(sem.t2, 1)
        ve.wait_ge(sem.t1, 1)
        ve.wait_ge(sem.a_f0, n_off)
        ve.tensor_tensor(T.ybuf[:, hs(0)], T.psOE[:, 0:HH, 0], T.fland[:, hs(0)], AluOpType.add).then_inc(sem.fin0, 1)
        ve.wait_ge(sem.t2, 1)
        ve.wait_ge(sem.a_f1, n_off)
        ve.tensor_tensor(T.ybuf[:, hs(1)], T.acc[:], T.fland[:, hs(1)], AluOpType.add).then_inc(sem.fin1, 1)

    g.wait_ge(sem.c_s, 1)
    if is_rank:
        call(xfer(S, m_off, sem.a_d0, [T.ob_s[:]], T.dland[:, hs(0)]))
    else:
        g.wait_ge(sem.c_o, 1)
        call(xfer(S, m_off, sem.a_d1, [T.ob_s[:]], T.dland[:, hs(1)]),
             xfer(rc, m_c0, sem.a_o, [T.ob_o[:]], T.oland[:]))
    g.wait_ge(sem.c_d, 1)
    call(xfer(S_lane, m_off, sem.a_raw, [T.ob_d[:]], T.rawland[:]))
    g.wait_ge(sem.c_x, 1)
    g.wait_ge(sem.a_raw, n_off)
    call(xfer(X, m_off, sem.a_f1 if lane else sem.a_f0, [T.rawland[:], T.ob_x[:]], T.fland[:, hs(lane)], 1))

    if is_rank:
        for b, qu, f, st in ((0, g.sync, sem.fin0, sem.st_y0), (1, g.scalar, sem.fin1, sem.st_y1)):
            qu.wait_ge(f, 1)
            qu.dma_start(T.y[:, hw(b)], T.ybuf[:, hs(b)]).then_inc(st, 16)
            qu.wait_ge(st, 16)
    g.wait_ge(sem.lsem, sent[0])
